import numpy as np
import ml_dtypes


def mxq(x, axis, fmt="e4m3"):
    dtype, down = {"e4m3": (ml_dtypes.float8_e4m3fn, 7), "e5m2": (ml_dtypes.float8_e5m2, 14)}[fmt]
    v = np.moveaxis(np.asarray(x, np.float32).astype(ml_dtypes.bfloat16).astype(np.float64), axis, -1)
    blocks = v.reshape(v.shape[:-1] + (-1, 32))
    amax = np.abs(blocks).max(-1, keepdims=True)
    byte = np.maximum(np.where(amax > 0, np.frexp(amax)[1] - 1 + 127, 0) - down, 1)
    scale = np.exp2(byte - 127.0)
    codes = (blocks / scale).astype(np.float32).astype(dtype).astype(np.float64)
    return np.moveaxis((codes * scale).reshape(v.shape), -1, axis)


WIDE = False


def mx_kscale(k):
    if not WIDE:
        return np.ones(k)
    levels = np.array([10, -10, 5, -5, 0])
    if k % 512:
        return np.exp2(np.random.permutation(np.resize(levels, k // 32))).repeat(32)
    a = np.empty((k // 512, 16))
    for p in range(k // 512):
        a[p, :8] = np.random.permutation(np.resize(levels, 8))
        for g in range(8):
            far = levels[np.abs(levels - a[p, g]) >= 10]
            a[p, g + 8] = far[np.random.randint(len(far))]
    return np.exp2(a.ravel()).repeat(32)


def f64(x):
    return np.asarray(x).astype(np.float64)


def striped(idx):
    return np.tile(np.asarray(idx).reshape(-1, 16).T, (8, 1)).astype(np.uint16)


def unstriped(offs):
    return offs[:16].T.reshape(-1).astype(np.int64)


B, N, T, D, DV, NQ = 2, 512, 2048, 512, 256, 256
PAGE = 64
CAP = 2.0


def setup_inputs():
    n = np.random.standard_normal
    pages = np.random.permutation(T // PAGE)[:B * N // PAGE]
    idx = (pages[:, None] * PAGE + np.arange(PAGE)[None, :]).reshape(-1)
    s = mx_kscale(D)[:, None]
    u = np.ones(T)
    u[idx] = mx_kscale(B * N)
    r = np.random.uniform(0.5, 2.0, T)
    rk = np.random.uniform(0.5, 2.0, T)
    k = n((D, T)) / s / rk
    v = n((DV, T)) / (u * r)
    return {
        "qT": (n((B, D, NQ)) * s * (0.80 / np.sqrt(D))).astype(np.float32),
        "kT": k.astype(np.float32),
        "vT": v.astype(np.float32),
        "ks": np.tile(rk, (128, 1)).astype(np.float32),
        "vs": np.tile(u * r, (128, 1)).astype(np.float32),
        "offs": striped(idx),
    }


def reference(qT, kT, vT, ks, vs, offs):
    idx = unstriped(offs)
    k = f64(kT)
    v = f64(vT)
    pick = lambda x: x[:, idx].reshape(x.shape[0], B, N).transpose(1, 0, 2)
    q = f64(qT)
    score = mxq(q, 1, "e4m3").transpose(0, 2, 1) @ mxq(pick(k), 1, "e4m3")
    score = score * pick(f64(ks))[:, :1, :]
    score = CAP * np.tanh(score / CAP)
    m = score.max(-1, keepdims=True)
    p = np.exp(score - m)
    total = p.sum(-1, keepdims=True)
    w = p * pick(f64(vs))[:, :1, :]
    y = mxq(w, 2, "e4m3") @ mxq(pick(v).transpose(0, 2, 1), 1, "e4m3")
    y = y / total
    return y

@@ -1,0 +1,260 @@
+from contextlib import ExitStack
+
+import concourse.mybir as mybir
+from concourse.masks import make_identity
+
+B, N, T, D, DV, NQ = 2, 512, 2048, 512, 256, 256
+P = 128
+PACK = 4
+CAP = 2.0
+
+FLOPS = 2 * B * NQ * N * (D + DV)
+BYTES = 4 * (B * D * NQ + D * T + DV * T + 2 * T + B * NQ * DV) + 2 * B * N * P // 16
+
+F32 = mybir.dt.float32
+BF16 = mybir.dt.bfloat16
+U32 = mybir.dt.uint32
+U16 = mybir.dt.uint16
+U8 = mybir.dt.uint8
+FP8X4 = mybir.dt.float8_e4m3fn_x4
+
+MULT = mybir.AluOpType.mult
+MIN = mybir.AluOpType.min
+COPY = mybir.ActivationFunctionType.Copy
+EXP = mybir.ActivationFunctionType.Exp
+TANH = mybir.ActivationFunctionType.Tanh
+
+
+def tile_attend_x_ks_cap_kernel(tc, qT, kT, vT, ks, vs, offs, out):
+    nc = tc.nc
+    with ExitStack() as ctx:
+        held = ctx.enter_context(tc.tile_pool(name="held", bufs=1))
+        work = ctx.enter_context(tc.tile_pool(name="work", bufs=2))
+        psum = ctx.enter_context(tc.psum_pool(name="psum", bufs=2))
+
+        offsets = held.tile([P, B * N // 16], U16, name="offsets")
+        nc.sync.dma_start(offsets[:], offs)
+        ks_pool = held.tile([P, T], F32, name="ks_pool")
+        vs_pool = held.tile([P, T], F32, name="vs_pool")
+        nc.vector.memset(ks_pool[:], 0.0)
+        nc.gpsimd.memset(vs_pool[:], 0.0)
+        nc.scalar.dma_start(ks_pool[0:1, :], ks[0:1, :])
+        nc.scalar.dma_start(vs_pool[0:1, :], vs[0:1, :])
+        warm = held.tile([P, 8], F32, name="warm")
+        nc.vector.memset(warm[:], 0.0)
+        nc.scalar.activation(warm[:, 0:1], warm[:, 1:2], EXP)
+        ident_f = held.tile([P, P], F32, name="ident_f")
+        make_identity(nc, ident_f[:])
+        ident_b = held.tile([P, P], BF16, name="ident_b")
+        make_identity(nc, ident_b[:])
+
+        q_raw = []
+        for b in range(B):
+            q_raw.append(held.tile([P, PACK, NQ], F32, name=f"q_raw{b}"))
+        k_pool = []
+        for j in range(PACK):
+            k_pool.append(held.tile([P, T], F32, name=f"k_pool{j}"))
+        v_pool = []
+        for h in range(2):
+            v_pool.append(held.tile([P, T], F32, name=f"v_pool{h}"))
+        k_rows = kT.rearrange("(p j) w -> p j w", j=PACK)
+        nc.sync.dma_start(q_raw[0][:], qT[0].rearrange("(p j) w -> p j w", j=PACK))
+        for j in range(PACK):
+            nc.sync.dma_start(k_pool[j][:], k_rows[:, j, :])
+        nc.sync.dma_start(q_raw[1][:], qT[1].rearrange("(p j) w -> p j w", j=PACK))
+        for h in range(2):
+            nc.sync.dma_start(v_pool[h][:], vT[h * P : (h + 1) * P, :])
+
+        ks_got = held.tile([P, B * N], F32, name="ks_got")
+        vs_got = held.tile([P, B * N], F32, name="vs_got")
+        nc.vector.tensor_copy(ks_got[:], ks_pool[:].indirect(offsets[:]))
+        nc.vector.tensor_copy(vs_got[:], vs_pool[:].indirect(offsets[:]))
+        ks_col = held.tile([P, 8], F32, name="ks_col")
+        vs_col = held.tile([P, 8], F32, name="vs_col")
+        vs_row = held.tile([P, B * N], F32, name="vs_row")
+        for got, col, factor in ((ks_got, ks_col, 1.0 / CAP), (vs_got, vs_col, 1.0)):
+            for b in range(B):
+                turned = psum.tile([P, 4, P], F32, name="turned", tag="tT")
+                for m in range(4):
+                    nc.tensor.transpose(turned[:, m, :], got[:, (4 * b + m) * P : (4 * b + m + 1) * P], ident_f[:])
+                nc.scalar.activation(col[:, 4 * b : 4 * b + 4], turned[:, :, 0], COPY, scale=factor)
+        for b in range(B):
+            spread = psum.tile([P, 4, P], F32, name="spread", tag="tT")
+            for m in range(4):
+                nc.tensor.transpose(spread[:, m, :], vs_col[:, 4 * b + m : 4 * b + m + 1].to_broadcast([P, P]), ident_f[:])
+            nc.scalar.copy(vs_row[:, b * N : (b + 1) * N], spread[:].rearrange("p m s -> p (m s)"))
+
+        q_codes, q_scales = [], []
+        k_codes, k_scales = [], []
+        w_codes, w_scales = [], []
+        v_codes, v_scales = [], []
+        for b in range(B):
+            q_codes.append(held.tile([P, NQ], U32, name=f"q_codes{b}", align_bytes=64))
+            q_scales.append(held.tile([P, NQ], U8, name=f"q_scales{b}", align_bytes=64))
+            k_codes.append(held.tile([P, N], U32, name=f"k_codes{b}", align_bytes=64))
+            k_scales.append(held.tile([P, N], U8, name=f"k_scales{b}", align_bytes=64))
+            w_codes.append(held.tile([P, NQ], U32, name=f"w_codes{b}", align_bytes=64))
+            w_scales.append(held.tile([P, NQ], U8, name=f"w_scales{b}", align_bytes=64))
+            v_codes.append(held.tile([P, DV], U32, name=f"v_codes{b}", align_bytes=64))
+            v_scales.append(held.tile([P, DV], U8, name=f"v_scales{b}", align_bytes=64))
+
+        def quantize(codes, scales, cols, grouped):
+            nc.vector.quantize_mx(
+                out=codes[:, cols].bitcast(FP8X4),
+                scales=scales[:, cols],
+                in_=grouped.rearrange("p c j -> p (c j)"),
+            )
+
+        q_in = []
+        for b in range(B):
+            q_in.append(held.tile([P, NQ, PACK], BF16, name=f"q_in{b}", align_bytes=64))
+
+        def group_q(b):
+            nc.scalar.copy(q_in[b][:], q_raw[b][:].rearrange("p j c -> p c j"))
+
+        def quant_q(b):
+            quantize(q_codes[b], q_scales[b], slice(0, NQ), q_in[b][:])
+
+        k_got = held.tile([P, PACK, B * N], F32, name="k_got")
+        k_in = []
+        for b in range(B):
+            k_in.append(held.tile([P, N, PACK], BF16, name=f"k_in{b}", align_bytes=64))
+
+        def gather_k(j, b):
+            nc.vector.tensor_copy(
+                k_got[:, j, b * N : (b + 1) * N],
+                k_pool[j][:].indirect(offsets[:, b * (N // 16) : (b + 1) * (N // 16)]),
+            )
+
+        def group_k(b):
+            half = N // 2
+            for engine, lo in ((nc.vector.tensor_copy, 0), (nc.scalar.copy, half)):
+                engine(
+                    k_in[b][:, lo : lo + half, :],
+                    k_got[:, :, b * N + lo : b * N + lo + half].rearrange("p j c -> p c j"),
+                )
+
+        def quant_k(b):
+            quantize(k_codes[b], k_scales[b], slice(0, N), k_in[b][:])
+
+        group_q(0)
+        quant_q(0)
+        for j in range(3):
+            for b in range(B):
+                gather_k(j, b)
+        for b in range(B):
+            gather_k(3, b)
+            group_k(b)
+        group_q(1)
+        quant_k(0)
+
+        v_got = []
+        for h in range(2):
+            v_got.append(held.tile([P, B * N], F32, name=f"v_got{h}"))
+        v_in, out_ps, rl = [], [], []
+        for b in range(B):
+            v_in.append(held.tile([P, DV, PACK], BF16, name=f"v_in{b}", align_bytes=64))
+            rl.append(held.tile([P, 2], F32, name=f"rl{b}"))
+            out_ps.append(psum.tile([P, 2, DV], F32, name="out_ps", tag="O", bufs=2))
+
+        def scores(b):
+            th = work.tile([P, 4, NQ], F32, name="th")
+            for g in range(2):
+                s_ps = psum.tile([P, 2, NQ], F32, name="s_ps", tag="S", bufs=2)
+                for i in range(2):
+                    m = 2 * g + i
+                    cols = slice(m * P, (m + 1) * P)
+                    nc.tensor.matmul_mx(
+                        out=s_ps[:, i, :],
+                        lhsT=k_codes[b][:, cols].bitcast(FP8X4),
+                        lhsT_scale=k_scales[b][:, cols],
+                        rhs=q_codes[b][:].bitcast(FP8X4),
+                        rhs_scale=q_scales[b][:],
+                        start=True,
+                        stop=True,
+                    )
+                    nc.scalar.activation(th[:, m, :], s_ps[:, i, :], TANH, scale=ks_col[:, 4 * b + m : 4 * b + m + 1])
+            return th
+
+        def soften(b, qt, th):
+            tT = psum.tile([P, N], F32, name="tT", tag="tT")
+            for m in range(4):
+                nc.tensor.transpose(tT[:, m * P : (m + 1) * P], th[:, m, qt * P : (qt + 1) * P], ident_f[:])
+            minus_c = work.tile([P, N], F32, name="minus_c")
+            minus_m = work.tile([P, 1], F32, name="minus_m")
+            nc.vector.tensor_scalar(minus_c[:], tT[:], -CAP, None, MULT, MIN, accum_out=minus_m[:])
+            p = work.tile([P, N], F32, name="p")
+            total = work.tile([P, 1], F32, name="total")
+            nc.scalar.activation(p[:], tT[:], EXP, bias=minus_m[:], scale=CAP, accum_out=total[:])
+            w = work.tile([P, N], BF16, name="w")
+            nc.vector.tensor_tensor(w[:], p[:], vs_row[:, b * N : (b + 1) * N], MULT)
+            nc.vector.reciprocal(rl[b][:, qt : qt + 1], total[:])
+            return w
+
+        def turn_w(b, qt, w):
+            wT = psum.tile([P, PACK, P], BF16, name="wT", tag="wT", bufs=1)
+            for t in range(PACK):
+                nc.tensor.transpose(wT[:, t, :], w[:, t::PACK], ident_b[:])
+            w_in = work.tile([P, P, PACK], BF16, name="w_in", align_bytes=64)
+            nc.scalar.copy(w_in[:], wT[:].rearrange("p t c -> p c t"))
+            quantize(w_codes[b], w_scales[b], slice(qt * P, (qt + 1) * P), w_in[:])
+
+        def value(h, b):
+            nc.vector.tensor_copy(
+                v_got[h][:, b * N : (b + 1) * N],
+                v_pool[h][:].indirect(offsets[:, b * (N // 16) : (b + 1) * (N // 16)]),
+            )
+            vT_ps = psum.tile([P, PACK, P], F32, name="vT_ps", tag="vT", bufs=1)
+            for t in range(PACK):
+                nc.tensor.transpose(vT_ps[:, t, :], v_got[h][:, b * N + t : (b + 1) * N : PACK], ident_f[:])
+            nc.scalar.copy(v_in[b][:, h * P : (h + 1) * P, :], vT_ps[:].rearrange("p t c -> p c t"))
+
+        def quant_v(h, b):
+            quantize(v_codes[b], v_scales[b], slice(h * P, (h + 1) * P), v_in[b][:, h * P : (h + 1) * P, :])
+
+        y = []
+        for b in range(B):
+            y.append(held.tile([P, 2, DV], F32, name=f"y{b}"))
+
+        def product(h, b):
+            cols = slice(h * P, (h + 1) * P)
+            for qt in range(2):
+                rows = slice(qt * P, (qt + 1) * P)
+                nc.tensor.matmul_mx(
+                    out=out_ps[b][:, qt, cols],
+                    lhsT=w_codes[b][:, rows].bitcast(FP8X4),
+                    lhsT_scale=w_scales[b][:, rows],
+                    rhs=v_codes[b][:, cols].bitcast(FP8X4),
+                    rhs_scale=v_scales[b][:, cols],
+                    start=True,
+                    stop=True,
+                )
+            for qt in range(2):
+                if qt == 0:
+                    nc.vector.tensor_scalar(y[b][:, qt, cols], out_ps[b][:, qt, cols], rl[b][:, qt : qt + 1], None, MULT)
+                else:
+                    nc.scalar.activation(y[b][:, qt, cols], out_ps[b][:, qt, cols], COPY, scale=rl[b][:, qt : qt + 1])
+
+        th0 = scores(0)
+        quant_k(1)
+        quant_q(1)
+        w00 = soften(0, 0, th0)
+        w01 = soften(0, 1, th0)
+        th1 = scores(1)
+        turn_w(0, 0, w00)
+        turn_w(0, 1, w01)
+        value(0, 0)
+        value(0, 1)
+        w10 = soften(1, 0, th1)
+        w11 = soften(1, 1, th1)
+        quant_v(0, 0)
+        quant_v(0, 1)
+        product(0, 0)
+        turn_w(1, 0, w10)
+        turn_w(1, 1, w11)
+        product(0, 1)
+        for b in range(B):
+            value(1, b)
+            quant_v(1, b)
+            product(1, b)
+            nc.sync.dma_start(out[b].rearrange("(t p) e -> p t e", p=P), y[b][:])

@@ -20,6 +20,7 @@ FP8X4 = mybir.dt.float8_e4m3fn_x4
 
 MULT = mybir.AluOpType.mult
 MIN = mybir.AluOpType.min
+ADD = mybir.AluOpType.add
 COPY = mybir.ActivationFunctionType.Copy
 EXP = mybir.ActivationFunctionType.Exp
 TANH = mybir.ActivationFunctionType.Tanh
@@ -34,61 +35,49 @@ def tile_attend_x_ks_cap_kernel(tc, qT, kT, vT, ks, vs, offs, out):
 
         offsets = held.tile([P, B * N // 16], U16, name="offsets")
         nc.sync.dma_start(offsets[:], offs)
+
         ks_pool = held.tile([P, T], F32, name="ks_pool")
         vs_pool = held.tile([P, T], F32, name="vs_pool")
         nc.vector.memset(ks_pool[:], 0.0)
-        nc.gpsimd.memset(vs_pool[:], 0.0)
-        nc.scalar.dma_start(ks_pool[0:1, :], ks[0:1, :])
-        nc.scalar.dma_start(vs_pool[0:1, :], vs[0:1, :])
         warm = held.tile([P, 8], F32, name="warm")
         nc.vector.memset(warm[:], 0.0)
+        nc.vector.memset(vs_pool[:], 0.0)
         nc.scalar.activation(warm[:, 0:1], warm[:, 1:2], EXP)
         ident_f = held.tile([P, P], F32, name="ident_f")
         make_identity(nc, ident_f[:])
         ident_b = held.tile([P, P], BF16, name="ident_b")
         make_identity(nc, ident_b[:])
 
-        q_raw = []
+        q_raw, k_pool, v_pool = [], [], []
         for b in range(B):
             q_raw.append(held.tile([P, PACK, NQ], F32, name=f"q_raw{b}"))
-        k_pool = []
         for j in range(PACK):
             k_pool.append(held.tile([P, T], F32, name=f"k_pool{j}"))
-        v_pool = []
         for h in range(2):
             v_pool.append(held.tile([P, T], F32, name=f"v_pool{h}"))
         k_rows = kT.rearrange("(p j) w -> p j w", j=PACK)
-        nc.sync.dma_start(q_raw[0][:], qT[0].rearrange("(p j) w -> p j w", j=PACK))
-        for j in range(PACK):
+        nc.sync.dma_start(k_pool[0][:], k_rows[:, 0, :])
+        nc.sync.dma_start(ks_pool[0:1, :], ks[0:1, :])
+        nc.sync.dma_start(k_pool[1][:], k_rows[:, 1, :])
+        nc.sync.dma_start(vs_pool[0:1, :], vs[0:1, :])
+        for j in range(2, PACK):
             nc.sync.dma_start(k_pool[j][:], k_rows[:, j, :])
-        nc.sync.dma_start(q_raw[1][:], qT[1].rearrange("(p j) w -> p j w", j=PACK))
+        for b in range(B):
+            nc.sync.dma_start(q_raw[b][:], qT[b].rearrange("(p j) w -> p j w", j=PACK))
         for h in range(2):
             nc.sync.dma_start(v_pool[h][:], vT[h * P : (h + 1) * P, :])
-
-        ks_got = held.tile([P, B * N], F32, name="ks_got")
-        vs_got = held.tile([P, B * N], F32, name="vs_got")
-        nc.vector.tensor_copy(ks_got[:], ks_pool[:].indirect(offsets[:]))
-        nc.vector.tensor_copy(vs_got[:], vs_pool[:].indirect(offsets[:]))
-        ks_col = held.tile([P, 8], F32, name="ks_col")
-        vs_col = held.tile([P, 8], F32, name="vs_col")
-        vs_row = held.tile([P, B * N], F32, name="vs_row")
-        for got, col, factor in ((ks_got, ks_col, 1.0 / CAP), (vs_got, vs_col, 1.0)):
-            for b in range(B):
-                turned = psum.tile([P, 4, P], F32, name="turned", tag="tT")
-                for m in range(4):
-                    nc.tensor.transpose(turned[:, m, :], got[:, (4 * b + m) * P : (4 * b + m + 1) * P], ident_f[:])
-                nc.scalar.activation(col[:, 4 * b : 4 * b + 4], turned[:, :, 0], COPY, scale=factor)
-        for b in range(B):
-            spread = psum.tile([P, 4, P], F32, name="spread", tag="tT")
-            for m in range(4):
-                nc.tensor.transpose(spread[:, m, :], vs_col[:, 4 * b + m : 4 * b + m + 1].to_broadcast([P, P]), ident_f[:])
-            nc.scalar.copy(vs_row[:, b * N : (b + 1) * N], spread[:].rearrange("p m s -> p (m s)"))
 
         q_codes, q_scales = [], []
         k_codes, k_scales = [], []
         w_codes, w_scales = [], []
         v_codes, v_scales = [], []
+        q_in, k_in, v_in, w_in = [], [], [], []
+        out_ps, total, inverse, y = [], [], [], []
         for b in range(B):
+            q_in.append(held.tile([P, NQ, PACK], BF16, name=f"q_in{b}", align_bytes=64))
+            k_in.append(held.tile([P, N, PACK], BF16, name=f"k_in{b}", align_bytes=64))
+            v_in.append(held.tile([P, DV, PACK], BF16, name=f"v_in{b}", align_bytes=64))
+            w_in.append(held.tile([P, NQ, PACK], BF16, name=f"w_in{b}", align_bytes=64))
             q_codes.append(held.tile([P, NQ], U32, name=f"q_codes{b}", align_bytes=64))
             q_scales.append(held.tile([P, NQ], U8, name=f"q_scales{b}", align_bytes=64))
             k_codes.append(held.tile([P, N], U32, name=f"k_codes{b}", align_bytes=64))
@@ -97,65 +86,52 @@ def tile_attend_x_ks_cap_kernel(tc, qT, kT, vT, ks, vs, offs, out):
             w_scales.append(held.tile([P, NQ], U8, name=f"w_scales{b}", align_bytes=64))
             v_codes.append(held.tile([P, DV], U32, name=f"v_codes{b}", align_bytes=64))
             v_scales.append(held.tile([P, DV], U8, name=f"v_scales{b}", align_bytes=64))
+            total.append(held.tile([P, 2], F32, name=f"total{b}"))
+            inverse.append(held.tile([P, 2], F32, name=f"inverse{b}"))
+            y.append(held.tile([P, 2, DV], F32, name=f"y{b}"))
+            out_ps.append(psum.tile([P, 2, DV], F32, name=f"out_ps{b}", tag="O", bufs=2))
+        ks_got = held.tile([P, B * N], F32, name="ks_got")
+        vs_got = held.tile([P, B * N], F32, name="vs_got")
+        ks_col = held.tile([P, 8], F32, name="ks_col")
+        vs_col = held.tile([P, 8], F32, name="vs_col")
+        vs_row = held.tile([P, B * N], F32, name="vs_row")
+        k_got = held.tile([P, PACK, B * N], F32, name="k_got")
+        v_got = []
+        for h in range(2):
+            v_got.append(held.tile([P, B * N], F32, name=f"v_got{h}"))
+
+        def slots(b):
+            return slice(b * N, (b + 1) * N)
+
+        def entries(b):
+            return offsets[:, b * (N // 16) : (b + 1) * (N // 16)]
 
         def quantize(codes, scales, cols, grouped):
             nc.vector.quantize_mx(
                 out=codes[:, cols].bitcast(FP8X4),
                 scales=scales[:, cols],
-                in_=grouped.rearrange("p c j -> p (c j)"),
+                in_=grouped[:, cols, :].rearrange("p c j -> p (c j)"),
             )
 
-        q_in = []
-        for b in range(B):
-            q_in.append(held.tile([P, NQ, PACK], BF16, name=f"q_in{b}", align_bytes=64))
+        def columns(got, col, factor):
+            for b in range(B):
+                turned = psum.tile([P, 4, P], F32, name="turned", tag="tT")
+                for m in range(4):
+                    nc.tensor.transpose(turned[:, m, :], got[:, (4 * b + m) * P : (4 * b + m + 1) * P], ident_f[:])
+                nc.scalar.activation(col[:, 4 * b : 4 * b + 4], turned[:, :, 0], COPY, scale=factor)
+
+        def spread_vs():
+            for b in range(B):
+                spread = psum.tile([P, 4, P], F32, name="spread", tag="tT")
+                for m in range(4):
+                    nc.tensor.transpose(spread[:, m, :], vs_col[:, 4 * b + m : 4 * b + m + 1].to_broadcast([P, P]), ident_f[:])
+                nc.scalar.copy(vs_row[:, slots(b)], spread[:].rearrange("p m s -> p (m s)"))
 
         def group_q(b):
-            nc.scalar.copy(q_in[b][:], q_raw[b][:].rearrange("p j c -> p c j"))
+            nc.gpsimd.tensor_scalar(q_in[b][:], q_raw[b][:].rearrange("p j c -> p c j"), 1.0, 0.0, MULT, ADD)
 
-        def quant_q(b):
-            quantize(q_codes[b], q_scales[b], slice(0, NQ), q_in[b][:])
-
-        k_got = held.tile([P, PACK, B * N], F32, name="k_got")
-        k_in = []
-        for b in range(B):
-            k_in.append(held.tile([P, N, PACK], BF16, name=f"k_in{b}", align_bytes=64))
-
-        def gather_k(j, b):
-            nc.vector.tensor_copy(
-                k_got[:, j, b * N : (b + 1) * N],
-                k_pool[j][:].indirect(offsets[:, b * (N // 16) : (b + 1) * (N // 16)]),
-            )
-
-        def group_k(b):
-            half = N // 2
-            for engine, lo in ((nc.vector.tensor_copy, 0), (nc.scalar.copy, half)):
-                engine(
-                    k_in[b][:, lo : lo + half, :],
-                    k_got[:, :, b * N + lo : b * N + lo + half].rearrange("p j c -> p c j"),
-                )
-
-        def quant_k(b):
-            quantize(k_codes[b], k_scales[b], slice(0, N), k_in[b][:])
-
-        group_q(0)
-        quant_q(0)
-        for j in range(3):
-            for b in range(B):
-                gather_k(j, b)
-        for b in range(B):
-            gather_k(3, b)
-            group_k(b)
-        group_q(1)
-        quant_k(0)
-
-        v_got = []
-        for h in range(2):
-            v_got.append(held.tile([P, B * N], F32, name=f"v_got{h}"))
-        v_in, out_ps, rl = [], [], []
-        for b in range(B):
-            v_in.append(held.tile([P, DV, PACK], BF16, name=f"v_in{b}", align_bytes=64))
-            rl.append(held.tile([P, 2], F32, name=f"rl{b}"))
-            out_ps.append(psum.tile([P, 2, DV], F32, name="out_ps", tag="O", bufs=2))
+        def group_k(engine, b, j):
+            engine(k_in[b][:, :, j : j + 2], k_got[:, j : j + 2, slots(b)].rearrange("p j c -> p c j"))
 
         def scores(b):
             th = work.tile([P, 4, NQ], F32, name="th")
@@ -176,52 +152,46 @@ def tile_attend_x_ks_cap_kernel(tc, qT, kT, vT, ks, vs, offs, out):
                     nc.scalar.activation(th[:, m, :], s_ps[:, i, :], TANH, scale=ks_col[:, 4 * b + m : 4 * b + m + 1])
             return th
 
-        def soften(b, qt, th):
+        def soften(b, t, th):
             tT = psum.tile([P, N], F32, name="tT", tag="tT")
             for m in range(4):
-                nc.tensor.transpose(tT[:, m * P : (m + 1) * P], th[:, m, qt * P : (qt + 1) * P], ident_f[:])
+                nc.tensor.transpose(tT[:, m * P : (m + 1) * P], th[:, m, t * P : (t + 1) * P], ident_f[:])
             minus_c = work.tile([P, N], F32, name="minus_c")
             minus_m = work.tile([P, 1], F32, name="minus_m")
             nc.vector.tensor_scalar(minus_c[:], tT[:], -CAP, None, MULT, MIN, accum_out=minus_m[:])
             p = work.tile([P, N], F32, name="p")
-            total = work.tile([P, 1], F32, name="total")
-            nc.scalar.activation(p[:], tT[:], EXP, bias=minus_m[:], scale=CAP, accum_out=total[:])
+            nc.scalar.activation(p[:], tT[:], EXP, bias=minus_m[:], scale=CAP, accum_out=total[b][:, t : t + 1])
+            return p
+
+        def weigh(b, t, p):
             w = work.tile([P, N], BF16, name="w")
-            nc.vector.tensor_tensor(w[:], p[:], vs_row[:, b * N : (b + 1) * N], MULT)
-            nc.vector.reciprocal(rl[b][:, qt : qt + 1], total[:])
-            return w
-
-        def turn_w(b, qt, w):
+            nc.vector.tensor_tensor(w[:], p[:], vs_row[:, slots(b)], MULT)
             wT = psum.tile([P, PACK, P], BF16, name="wT", tag="wT", bufs=1)
-            for t in range(PACK):
-                nc.tensor.transpose(wT[:, t, :], w[:, t::PACK], ident_b[:])
-            w_in = work.tile([P, P, PACK], BF16, name="w_in", align_bytes=64)
-            nc.scalar.copy(w_in[:], wT[:].rearrange("p t c -> p c t"))
-            quantize(w_codes[b], w_scales[b], slice(qt * P, (qt + 1) * P), w_in[:])
+            for j in range(PACK):
+                nc.tensor.transpose(wT[:, j, :], w[:, j::PACK], ident_b[:])
+            nc.scalar.copy(w_in[b][:, t * P : (t + 1) * P, :], wT[:].rearrange("p j c -> p c j"))
 
-        def value(h, b):
-            nc.vector.tensor_copy(
-                v_got[h][:, b * N : (b + 1) * N],
-                v_pool[h][:].indirect(offsets[:, b * (N // 16) : (b + 1) * (N // 16)]),
-            )
+        def quant_w(b, t):
+            quantize(w_codes[b], w_scales[b], slice(t * P, (t + 1) * P), w_in[b])
+
+        def gather_v(h, b):
+            nc.vector.tensor_copy(v_got[h][:, slots(b)], v_pool[h][:].indirect(entries(b)))
+
+        def turn_v(h, b):
             vT_ps = psum.tile([P, PACK, P], F32, name="vT_ps", tag="vT", bufs=1)
-            for t in range(PACK):
-                nc.tensor.transpose(vT_ps[:, t, :], v_got[h][:, b * N + t : (b + 1) * N : PACK], ident_f[:])
-            nc.scalar.copy(v_in[b][:, h * P : (h + 1) * P, :], vT_ps[:].rearrange("p t c -> p c t"))
+            for j in range(PACK):
+                nc.tensor.transpose(vT_ps[:, j, :], v_got[h][:, b * N + j : (b + 1) * N : PACK], ident_f[:])
+            nc.scalar.copy(v_in[b][:, h * P : (h + 1) * P, :], vT_ps[:].rearrange("p j c -> p c j"))
 
         def quant_v(h, b):
-            quantize(v_codes[b], v_scales[b], slice(h * P, (h + 1) * P), v_in[b][:, h * P : (h + 1) * P, :])
-
-        y = []
-        for b in range(B):
-            y.append(held.tile([P, 2, DV], F32, name=f"y{b}"))
+            quantize(v_codes[b], v_scales[b], slice(h * P, (h + 1) * P), v_in[b])
 
         def product(h, b):
             cols = slice(h * P, (h + 1) * P)
-            for qt in range(2):
-                rows = slice(qt * P, (qt + 1) * P)
+            for t in range(2):
+                rows = slice(t * P, (t + 1) * P)
                 nc.tensor.matmul_mx(
-                    out=out_ps[b][:, qt, cols],
+                    out=out_ps[b][:, t, cols],
                     lhsT=w_codes[b][:, rows].bitcast(FP8X4),
                     lhsT_scale=w_scales[b][:, rows],
                     rhs=v_codes[b][:, cols].bitcast(FP8X4),
@@ -229,32 +199,57 @@ def tile_attend_x_ks_cap_kernel(tc, qT, kT, vT, ks, vs, offs, out):
                     start=True,
                     stop=True,
                 )
-            for qt in range(2):
-                if qt == 0:
-                    nc.vector.tensor_scalar(y[b][:, qt, cols], out_ps[b][:, qt, cols], rl[b][:, qt : qt + 1], None, MULT)
-                else:
-                    nc.scalar.activation(y[b][:, qt, cols], out_ps[b][:, qt, cols], COPY, scale=rl[b][:, qt : qt + 1])
+            nc.vector.tensor_scalar(y[b][:, 0, cols], out_ps[b][:, 0, cols], inverse[b][:, 0:1], None, MULT)
+            nc.scalar.activation(y[b][:, 1, cols], out_ps[b][:, 1, cols], COPY, scale=inverse[b][:, 1:2])
 
-        th0 = scores(0)
-        quant_k(1)
-        quant_q(1)
-        w00 = soften(0, 0, th0)
-        w01 = soften(0, 1, th0)
-        th1 = scores(1)
-        turn_w(0, 0, w00)
-        turn_w(0, 1, w01)
-        value(0, 0)
-        value(0, 1)
-        w10 = soften(1, 0, th1)
-        w11 = soften(1, 1, th1)
-        quant_v(0, 0)
-        quant_v(0, 1)
-        product(0, 0)
-        turn_w(1, 0, w10)
-        turn_w(1, 1, w11)
-        product(0, 1)
+        nc.vector.tensor_copy(k_got[:, 0, :], k_pool[0][:].indirect(offsets[:]))
+        nc.vector.tensor_copy(ks_got[:], ks_pool[:].indirect(offsets[:]))
+        nc.vector.tensor_copy(k_got[:, 1, :], k_pool[1][:].indirect(offsets[:]))
+        columns(ks_got, ks_col, 1.0 / CAP)
         for b in range(B):
-            value(1, b)
-            quant_v(1, b)
-            product(1, b)
-            nc.sync.dma_start(out[b].rearrange("(t p) e -> p t e", p=P), y[b][:])
+            group_k(nc.scalar.copy, b, 0)
+        nc.vector.tensor_copy(vs_got[:], vs_pool[:].indirect(offsets[:]))
+        columns(vs_got, vs_col, 1.0)
+        spread_vs()
+        nc.vector.tensor_copy(k_got[:, 2, :], k_pool[2][:].indirect(offsets[:]))
+        for b in range(B):
+            nc.vector.tensor_copy(k_got[:, 3, slots(b)], k_pool[3][:].indirect(entries(b)))
+            group_k(nc.vector.tensor_copy, b, 2)
+            group_q(b)
+        for b in range(B):
+            quantize(k_codes[b], k_scales[b], slice(0, N), k_in[b])
+            quantize(q_codes[b], q_scales[b], slice(0, NQ), q_in[b])
+        th0 = scores(0)
+        gather_v(0, 0)
+        p00 = soften(0, 0, th0)
+        p01 = soften(0, 1, th0)
+        th1 = scores(1)
+        turn_v(0, 0)
+        gather_v(0, 1)
+        weigh(0, 0, p00)
+        weigh(0, 1, p01)
+        nc.vector.reciprocal(inverse[0][:], total[0][:])
+        p10 = soften(1, 0, th1)
+        p11 = soften(1, 1, th1)
+        turn_v(0, 1)
+        quant_w(0, 0)
+        quant_v(0, 0)
+        quant_w(0, 1)
+        gather_v(1, 0)
+        weigh(1, 0, p10)
+        turn_v(1, 0)
+        product(0, 0)
+        quant_v(0, 1)
+        weigh(1, 1, p11)
+        nc.vector.reciprocal(inverse[1][:], total[1][:])
+        gather_v(1, 1)
+        quant_w(1, 0)
+        quant_v(1, 0)
+        turn_v(1, 1)
+        quant_w(1, 1)
+        product(1, 0)
+        nc.sync.dma_start(out[0].rearrange("(t p) e -> p t e", p=P), y[0][:])
+        product(0, 1)
+        quant_v(1, 1)
+        product(1, 1)
+        nc.sync.dma_start(out[1].rearrange("(t p) e -> p t e", p=P), y[1][:])

@@ -20,7 +20,6 @@ FP8X4 = mybir.dt.float8_e4m3fn_x4
 
 MULT = mybir.AluOpType.mult
 MIN = mybir.AluOpType.min
-ADD = mybir.AluOpType.add
 COPY = mybir.ActivationFunctionType.Copy
 EXP = mybir.ActivationFunctionType.Exp
 TANH = mybir.ActivationFunctionType.Tanh
@@ -128,7 +127,7 @@ def tile_attend_x_ks_cap_kernel(tc, qT, kT, vT, ks, vs, offs, out):
                 nc.scalar.copy(vs_row[:, slots(b)], spread[:].rearrange("p m s -> p (m s)"))
 
         def group_q(b):
-            nc.gpsimd.tensor_scalar(q_in[b][:], q_raw[b][:].rearrange("p j c -> p c j"), 1.0, 0.0, MULT, ADD)
+            nc.scalar.copy(q_in[b][:], q_raw[b][:].rearrange("p j c -> p c j"))
 
         def group_k(engine, b, j):
             engine(k_in[b][:, :, j : j + 2], k_got[:, j : j + 2, slots(b)].rearrange("p j c -> p c j"))
@@ -186,70 +185,81 @@ def tile_attend_x_ks_cap_kernel(tc, qT, kT, vT, ks, vs, offs, out):
         def quant_v(h, b):
             quantize(v_codes[b], v_scales[b], slice(h * P, (h + 1) * P), v_in[b])
 
-        def product(h, b):
+        def product(h, b, t):
             cols = slice(h * P, (h + 1) * P)
-            for t in range(2):
-                rows = slice(t * P, (t + 1) * P)
-                nc.tensor.matmul_mx(
-                    out=out_ps[b][:, t, cols],
-                    lhsT=w_codes[b][:, rows].bitcast(FP8X4),
-                    lhsT_scale=w_scales[b][:, rows],
-                    rhs=v_codes[b][:, cols].bitcast(FP8X4),
-                    rhs_scale=v_scales[b][:, cols],
-                    start=True,
-                    stop=True,
-                )
-            nc.vector.tensor_scalar(y[b][:, 0, cols], out_ps[b][:, 0, cols], inverse[b][:, 0:1], None, MULT)
-            nc.scalar.activation(y[b][:, 1, cols], out_ps[b][:, 1, cols], COPY, scale=inverse[b][:, 1:2])
+            rows = slice(t * P, (t + 1) * P)
+            nc.tensor.matmul_mx(
+                out=out_ps[b][:, t, cols],
+                lhsT=w_codes[b][:, rows].bitcast(FP8X4),
+                lhsT_scale=w_scales[b][:, rows],
+                rhs=v_codes[b][:, cols].bitcast(FP8X4),
+                rhs_scale=v_scales[b][:, cols],
+                start=True,
+                stop=True,
+            )
+            if t == 0:
+                nc.vector.tensor_scalar(y[b][:, 0, cols], out_ps[b][:, 0, cols], inverse[b][:, 0:1], None, MULT)
+            else:
+                nc.scalar.activation(y[b][:, 1, cols], out_ps[b][:, 1, cols], COPY, scale=inverse[b][:, 1:2])
 
-        nc.vector.tensor_copy(k_got[:, 0, :], k_pool[0][:].indirect(offsets[:]))
+        def gather_k(j):
+            nc.vector.tensor_copy(k_got[:, j, :], k_pool[j][:].indirect(offsets[:]))
+
+        gather_k(0)
         nc.vector.tensor_copy(ks_got[:], ks_pool[:].indirect(offsets[:]))
-        nc.vector.tensor_copy(k_got[:, 1, :], k_pool[1][:].indirect(offsets[:]))
+        gather_k(1)
         columns(ks_got, ks_col, 1.0 / CAP)
         for b in range(B):
             group_k(nc.scalar.copy, b, 0)
         nc.vector.tensor_copy(vs_got[:], vs_pool[:].indirect(offsets[:]))
-        columns(vs_got, vs_col, 1.0)
-        spread_vs()
-        nc.vector.tensor_copy(k_got[:, 2, :], k_pool[2][:].indirect(offsets[:]))
+        gather_k(2)
         for b in range(B):
             nc.vector.tensor_copy(k_got[:, 3, slots(b)], k_pool[3][:].indirect(entries(b)))
-            group_k(nc.vector.tensor_copy, b, 2)
-            group_q(b)
-        for b in range(B):
-            quantize(k_codes[b], k_scales[b], slice(0, N), k_in[b])
-            quantize(q_codes[b], q_scales[b], slice(0, NQ), q_in[b])
+        group_k(nc.vector.tensor_copy, 0, 2)
+        group_q(0)
+        columns(vs_got, vs_col, 1.0)
+        spread_vs()
+        group_q(1)
+        quantize(k_codes[0], k_scales[0], slice(0, N), k_in[0])
+        quantize(q_codes[0], q_scales[0], slice(0, NQ), q_in[0])
         th0 = scores(0)
+        group_k(nc.vector.tensor_copy, 1, 2)
+        quantize(q_codes[1], q_scales[1], slice(0, NQ), q_in[1])
+        quantize(k_codes[1], k_scales[1], slice(0, N), k_in[1])
         gather_v(0, 0)
+        gather_v(0, 1)
+        th1 = scores(1)
         p00 = soften(0, 0, th0)
         p01 = soften(0, 1, th0)
-        th1 = scores(1)
         turn_v(0, 0)
-        gather_v(0, 1)
-        weigh(0, 0, p00)
-        weigh(0, 1, p01)
-        nc.vector.reciprocal(inverse[0][:], total[0][:])
-        p10 = soften(1, 0, th1)
-        p11 = soften(1, 1, th1)
-        turn_v(0, 1)
-        quant_w(0, 0)
-        quant_v(0, 0)
-        quant_w(0, 1)
         gather_v(1, 0)
+        weigh(0, 0, p00)
+        p10 = soften(1, 0, th1)
+        turn_v(0, 1)
+        weigh(0, 1, p01)
+        p11 = soften(1, 1, th1)
+        quant_w(0, 0)
+        nc.vector.reciprocal(inverse[0][:], total[0][:])
+        quant_v(0, 0)
         weigh(1, 0, p10)
         turn_v(1, 0)
-        product(0, 0)
-        quant_v(0, 1)
+        gather_v(1, 1)
+        quant_w(0, 1)
+        product(0, 0, 0)
+        product(0, 0, 1)
         weigh(1, 1, p11)
         nc.vector.reciprocal(inverse[1][:], total[1][:])
-        gather_v(1, 1)
-        quant_w(1, 0)
         quant_v(1, 0)
         turn_v(1, 1)
-        quant_w(1, 1)
-        product(1, 0)
+        product(1, 0, 0)
+        product(1, 0, 1)
         nc.sync.dma_start(out[0].rearrange("(t p) e -> p t e", p=P), y[0][:])
-        product(0, 1)
+        quant_w(1, 0)
+        quant_v(0, 1)
         quant_v(1, 1)
-        product(1, 1)
+        product(0, 1, 0)
+        product(1, 1, 0)
+        quant_w(1, 1)
+        product(0, 1, 1)
+        product(1, 1, 1)
         nc.sync.dma_start(out[1].rearrange("(t p) e -> p t e", p=P), y[1][:])

@@ -185,22 +185,22 @@ def tile_attend_x_ks_cap_kernel(tc, qT, kT, vT, ks, vs, offs, out):
         def quant_v(h, b):
             quantize(v_codes[b], v_scales[b], slice(h * P, (h + 1) * P), v_in[b])
 
-        def product(h, b, t):
-            cols = slice(h * P, (h + 1) * P)
+        def product(b, t):
             rows = slice(t * P, (t + 1) * P)
             nc.tensor.matmul_mx(
-                out=out_ps[b][:, t, cols],
+                out=out_ps[b][:, t, :],
                 lhsT=w_codes[b][:, rows].bitcast(FP8X4),
                 lhsT_scale=w_scales[b][:, rows],
-                rhs=v_codes[b][:, cols].bitcast(FP8X4),
-                rhs_scale=v_scales[b][:, cols],
+                rhs=v_codes[b][:].bitcast(FP8X4),
+                rhs_scale=v_scales[b][:],
                 start=True,
                 stop=True,
             )
-            if t == 0:
-                nc.vector.tensor_scalar(y[b][:, 0, cols], out_ps[b][:, 0, cols], inverse[b][:, 0:1], None, MULT)
+            if (b, t) == (1, 1):
+                nc.vector.tensor_scalar(y[b][:, t, :], out_ps[b][:, t, :], inverse[b][:, t : t + 1], None, MULT)
             else:
-                nc.scalar.activation(y[b][:, 1, cols], out_ps[b][:, 1, cols], COPY, scale=inverse[b][:, 1:2])
+                nc.scalar.activation(y[b][:, t, :], out_ps[b][:, t, :], COPY, scale=inverse[b][:, t : t + 1])
+            nc.sync.dma_start(out[b, rows, :], y[b][:, t, :])
 
         def gather_k(j):
             nc.vector.tensor_copy(k_got[:, j, :], k_pool[j][:].indirect(offsets[:]))
@@ -226,8 +226,7 @@ def tile_attend_x_ks_cap_kernel(tc, qT, kT, vT, ks, vs, offs, out):
         group_k(nc.vector.tensor_copy, 1, 2)
         quantize(q_codes[1], q_scales[1], slice(0, NQ), q_in[1])
         quantize(k_codes[1], k_scales[1], slice(0, N), k_in[1])
-        gather_v(0, 0)
-        gather_v(0, 1)
+        nc.vector.tensor_copy(v_got[0][:], v_pool[0][:].indirect(offsets[:]))
         th1 = scores(1)
         p00 = soften(0, 0, th0)
         p01 = soften(0, 1, th0)
@@ -238,28 +237,20 @@ def tile_attend_x_ks_cap_kernel(tc, qT, kT, vT, ks, vs, offs, out):
         turn_v(0, 1)
         weigh(0, 1, p01)
         p11 = soften(1, 1, th1)
-        quant_w(0, 0)
         nc.vector.reciprocal(inverse[0][:], total[0][:])
-        quant_v(0, 0)
         weigh(1, 0, p10)
         turn_v(1, 0)
         gather_v(1, 1)
-        quant_w(0, 1)
-        product(0, 0, 0)
-        product(0, 0, 1)
+        quantize(w_codes[0], w_scales[0], slice(0, NQ), w_in[0])
         weigh(1, 1, p11)
         nc.vector.reciprocal(inverse[1][:], total[1][:])
-        quant_v(1, 0)
+        quantize(v_codes[0], v_scales[0], slice(0, DV), v_in[0])
         turn_v(1, 1)
-        product(1, 0, 0)
-        product(1, 0, 1)
-        nc.sync.dma_start(out[0].rearrange("(t p) e -> p t e", p=P), y[0][:])
+        product(0, 0)
+        product(0, 1)
         quant_w(1, 0)
         quant_v(0, 1)
         quant_v(1, 1)
-        product(0, 1, 0)
-        product(1, 1, 0)
+        product(1, 0)
         quant_w(1, 1)
-        product(0, 1, 1)
-        product(1, 1, 1)
-        nc.sync.dma_start(out[1].rearrange("(t p) e -> p t e", p=P), y[1][:])
+        product(1, 1)

from contextlib import ExitStack

import concourse.mybir as mybir
from concourse.masks import make_identity

B, N, T, D, DV, NQ = 2, 512, 2048, 512, 256, 256
P = 128
PACK = 4
CAP = 2.0

FLOPS = 2 * B * NQ * N * (D + DV)
BYTES = 4 * (B * D * NQ + D * T + DV * T + 2 * T + B * NQ * DV) + 2 * B * N * P // 16

F32 = mybir.dt.float32
BF16 = mybir.dt.bfloat16
U32 = mybir.dt.uint32
U16 = mybir.dt.uint16
U8 = mybir.dt.uint8
FP8X4 = mybir.dt.float8_e4m3fn_x4

MULT = mybir.AluOpType.mult
MIN = mybir.AluOpType.min
COPY = mybir.ActivationFunctionType.Copy
EXP = mybir.ActivationFunctionType.Exp
TANH = mybir.ActivationFunctionType.Tanh


def tile_attend_x_ks_cap_kernel(tc, qT, kT, vT, ks, vs, offs, out):
    nc = tc.nc
    with ExitStack() as ctx:
        held = ctx.enter_context(tc.tile_pool(name="held", bufs=1))
        work = ctx.enter_context(tc.tile_pool(name="work", bufs=2))
        psum = ctx.enter_context(tc.psum_pool(name="psum", bufs=2))

        offsets = held.tile([P, B * N // 16], U16, name="offsets")
        nc.sync.dma_start(offsets[:], offs)

        ks_pool = held.tile([P, T], F32, name="ks_pool")
        vs_pool = held.tile([P, T], F32, name="vs_pool")
        nc.vector.memset(ks_pool[:], 0.0)
        warm = held.tile([P, 8], F32, name="warm")
        nc.vector.memset(warm[:], 0.0)
        nc.vector.memset(vs_pool[:], 0.0)
        nc.scalar.activation(warm[:, 0:1], warm[:, 1:2], EXP)
        ident_f = held.tile([P, P], F32, name="ident_f")
        make_identity(nc, ident_f[:])
        ident_b = held.tile([P, P], BF16, name="ident_b")
        make_identity(nc, ident_b[:])

        q_raw, k_pool, v_pool = [], [], []
        for b in range(B):
            q_raw.append(held.tile([P, PACK, NQ], F32, name=f"q_raw{b}"))
        for j in range(PACK):
            k_pool.append(held.tile([P, T], F32, name=f"k_pool{j}"))
        for h in range(2):
            v_pool.append(held.tile([P, T], F32, name=f"v_pool{h}"))
        k_rows = kT.rearrange("(p j) w -> p j w", j=PACK)
        nc.sync.dma_start(k_pool[0][:], k_rows[:, 0, :])
        nc.sync.dma_start(ks_pool[0:1, :], ks[0:1, :])
        nc.sync.dma_start(k_pool[1][:], k_rows[:, 1, :])
        nc.sync.dma_start(vs_pool[0:1, :], vs[0:1, :])
        for j in range(2, PACK):
            nc.sync.dma_start(k_pool[j][:], k_rows[:, j, :])
        for b in range(B):
            nc.sync.dma_start(q_raw[b][:], qT[b].rearrange("(p j) w -> p j w", j=PACK))
        for h in range(2):
            nc.sync.dma_start(v_pool[h][:], vT[h * P : (h + 1) * P, :])

        q_codes, q_scales = [], []
        k_codes, k_scales = [], []
        w_codes, w_scales = [], []
        v_codes, v_scales = [], []
        q_in, k_in, v_in, w_in = [], [], [], []
        out_ps, total, inverse, y = [], [], [], []
        for b in range(B):
            q_in.append(held.tile([P, NQ, PACK], BF16, name=f"q_in{b}", align_bytes=64))
            k_in.append(held.tile([P, N, PACK], BF16, name=f"k_in{b}", align_bytes=64))
            v_in.append(held.tile([P, DV, PACK], BF16, name=f"v_in{b}", align_bytes=64))
            w_in.append(held.tile([P, NQ, PACK], BF16, name=f"w_in{b}", align_bytes=64))
            q_codes.append(held.tile([P, NQ], U32, name=f"q_codes{b}", align_bytes=64))
            q_scales.append(held.tile([P, NQ], U8, name=f"q_scales{b}", align_bytes=64))
            k_codes.append(held.tile([P, N], U32, name=f"k_codes{b}", align_bytes=64))
            k_scales.append(held.tile([P, N], U8, name=f"k_scales{b}", align_bytes=64))
            w_codes.append(held.tile([P, NQ], U32, name=f"w_codes{b}", align_bytes=64))
            w_scales.append(held.tile([P, NQ], U8, name=f"w_scales{b}", align_bytes=64))
            v_codes.append(held.tile([P, DV], U32, name=f"v_codes{b}", align_bytes=64))
            v_scales.append(held.tile([P, DV], U8, name=f"v_scales{b}", align_bytes=64))
            total.append(held.tile([P, 2], F32, name=f"total{b}"))
            inverse.append(held.tile([P, 2], F32, name=f"inverse{b}"))
            y.append(held.tile([P, 2, DV], F32, name=f"y{b}"))
            out_ps.append(psum.tile([P, 2, DV], F32, name=f"out_ps{b}", tag="O", bufs=2))
        ks_got = held.tile([P, B * N], F32, name="ks_got")
        vs_got = held.tile([P, B * N], F32, name="vs_got")
        ks_col = held.tile([P, 8], F32, name="ks_col")
        vs_col = held.tile([P, 8], F32, name="vs_col")
        vs_row = held.tile([P, B * N], F32, name="vs_row")
        k_got = held.tile([P, PACK, B * N], F32, name="k_got")
        v_got = []
        for h in range(2):
            v_got.append(held.tile([P, B * N], F32, name=f"v_got{h}"))

        def slots(b):
            return slice(b * N, (b + 1) * N)

        def entries(b):
            return offsets[:, b * (N // 16) : (b + 1) * (N // 16)]

        def quantize(codes, scales, cols, grouped):
            nc.vector.quantize_mx(
                out=codes[:, cols].bitcast(FP8X4),
                scales=scales[:, cols],
                in_=grouped[:, cols, :].rearrange("p c j -> p (c j)"),
            )

        def columns(got, col, factor):
            for b in range(B):
                turned = psum.tile([P, 4, P], F32, name="turned", tag="tT")
                for m in range(4):
                    nc.tensor.transpose(turned[:, m, :], got[:, (4 * b + m) * P : (4 * b + m + 1) * P], ident_f[:])
                nc.scalar.activation(col[:, 4 * b : 4 * b + 4], turned[:, :, 0], COPY, scale=factor)

        def spread_vs():
            for b in range(B):
                spread = psum.tile([P, 4, P], F32, name="spread", tag="tT")
                for m in range(4):
                    nc.tensor.transpose(spread[:, m, :], vs_col[:, 4 * b + m : 4 * b + m + 1].to_broadcast([P, P]), ident_f[:])
                nc.scalar.copy(vs_row[:, slots(b)], spread[:].rearrange("p m s -> p (m s)"))

        def group_q(b):
            nc.scalar.copy(q_in[b][:], q_raw[b][:].rearrange("p j c -> p c j"))

        def group_k(engine, b, j):
            engine(k_in[b][:, :, j : j + 2], k_got[:, j : j + 2, slots(b)].rearrange("p j c -> p c j"))

        def scores(b):
            th = work.tile([P, 4, NQ], F32, name="th")
            for g in range(2):
                s_ps = psum.tile([P, 2, NQ], F32, name="s_ps", tag="S", bufs=2)
                for i in range(2):
                    m = 2 * g + i
                    cols = slice(m * P, (m + 1) * P)
                    nc.tensor.matmul_mx(
                        out=s_ps[:, i, :],
                        lhsT=k_codes[b][:, cols].bitcast(FP8X4),
                        lhsT_scale=k_scales[b][:, cols],
                        rhs=q_codes[b][:].bitcast(FP8X4),
                        rhs_scale=q_scales[b][:],
                        start=True,
                        stop=True,
                    )
                    nc.scalar.activation(th[:, m, :], s_ps[:, i, :], TANH, scale=ks_col[:, 4 * b + m : 4 * b + m + 1])
            return th

        def soften(b, t, th):
            tT = psum.tile([P, N], F32, name="tT", tag="tT")
            for m in range(4):
                nc.tensor.transpose(tT[:, m * P : (m + 1) * P], th[:, m, t * P : (t + 1) * P], ident_f[:])
            minus_c = work.tile([P, N], F32, name="minus_c")
            minus_m = work.tile([P, 1], F32, name="minus_m")
            nc.vector.tensor_scalar(minus_c[:], tT[:], -CAP, None, MULT, MIN, accum_out=minus_m[:])
            p = work.tile([P, N], F32, name="p")
            nc.scalar.activation(p[:], tT[:], EXP, bias=minus_m[:], scale=CAP, accum_out=total[b][:, t : t + 1])
            return p

        def weigh(b, t, p):
            w = work.tile([P, N], BF16, name="w")
            nc.vector.tensor_tensor(w[:], p[:], vs_row[:, slots(b)], MULT)
            wT = psum.tile([P, PACK, P], BF16, name="wT", tag="wT", bufs=1)
            for j in range(PACK):
                nc.tensor.transpose(wT[:, j, :], w[:, j::PACK], ident_b[:])
            nc.scalar.copy(w_in[b][:, t * P : (t + 1) * P, :], wT[:].rearrange("p j c -> p c j"))

        def quant_w(b, t):
            quantize(w_codes[b], w_scales[b], slice(t * P, (t + 1) * P), w_in[b])

        def gather_v(h, b):
            nc.vector.tensor_copy(v_got[h][:, slots(b)], v_pool[h][:].indirect(entries(b)))

        def turn_v(h, b):
            vT_ps = psum.tile([P, PACK, P], F32, name="vT_ps", tag="vT", bufs=1)
            for j in range(PACK):
                nc.tensor.transpose(vT_ps[:, j, :], v_got[h][:, b * N + j : (b + 1) * N : PACK], ident_f[:])
            nc.scalar.copy(v_in[b][:, h * P : (h + 1) * P, :], vT_ps[:].rearrange("p j c -> p c j"))

        def quant_v(h, b):
            quantize(v_codes[b], v_scales[b], slice(h * P, (h + 1) * P), v_in[b])

        def product(b, t):
            rows = slice(t * P, (t + 1) * P)
            nc.tensor.matmul_mx(
                out=out_ps[b][:, t, :],
                lhsT=w_codes[b][:, rows].bitcast(FP8X4),
                lhsT_scale=w_scales[b][:, rows],
                rhs=v_codes[b][:].bitcast(FP8X4),
                rhs_scale=v_scales[b][:],
                start=True,
                stop=True,
            )
            if (b, t) == (1, 1):
                nc.vector.tensor_scalar(y[b][:, t, :], out_ps[b][:, t, :], inverse[b][:, t : t + 1], None, MULT)
            else:
                nc.scalar.activation(y[b][:, t, :], out_ps[b][:, t, :], COPY, scale=inverse[b][:, t : t + 1])
            nc.sync.dma_start(out[b, rows, :], y[b][:, t, :])

        def gather_k(j):
            nc.vector.tensor_copy(k_got[:, j, :], k_pool[j][:].indirect(offsets[:]))

        gather_k(0)
        nc.vector.tensor_copy(ks_got[:], ks_pool[:].indirect(offsets[:]))
        gather_k(1)
        columns(ks_got, ks_col, 1.0 / CAP)
        for b in range(B):
            group_k(nc.scalar.copy, b, 0)
        nc.vector.tensor_copy(vs_got[:], vs_pool[:].indirect(offsets[:]))
        gather_k(2)
        for b in range(B):
            nc.vector.tensor_copy(k_got[:, 3, slots(b)], k_pool[3][:].indirect(entries(b)))
        group_k(nc.vector.tensor_copy, 0, 2)
        group_q(0)
        columns(vs_got, vs_col, 1.0)
        spread_vs()
        group_q(1)
        quantize(k_codes[0], k_scales[0], slice(0, N), k_in[0])
        quantize(q_codes[0], q_scales[0], slice(0, NQ), q_in[0])
        th0 = scores(0)
        group_k(nc.vector.tensor_copy, 1, 2)
        quantize(q_codes[1], q_scales[1], slice(0, NQ), q_in[1])
        quantize(k_codes[1], k_scales[1], slice(0, N), k_in[1])
        nc.vector.tensor_copy(v_got[0][:], v_pool[0][:].indirect(offsets[:]))
        th1 = scores(1)
        p00 = soften(0, 0, th0)
        p01 = soften(0, 1, th0)
        turn_v(0, 0)
        gather_v(1, 0)
        weigh(0, 0, p00)
        p10 = soften(1, 0, th1)
        turn_v(0, 1)
        weigh(0, 1, p01)
        p11 = soften(1, 1, th1)
        nc.vector.reciprocal(inverse[0][:], total[0][:])
        weigh(1, 0, p10)
        turn_v(1, 0)
        gather_v(1, 1)
        quantize(w_codes[0], w_scales[0], slice(0, NQ), w_in[0])
        weigh(1, 1, p11)
        nc.vector.reciprocal(inverse[1][:], total[1][:])
        quantize(v_codes[0], v_scales[0], slice(0, DV), v_in[0])
        turn_v(1, 1)
        product(0, 0)
        product(0, 1)
        quant_w(1, 0)
        quant_v(0, 1)
        quant_v(1, 1)
        product(1, 0)
        quant_w(1, 1)
        product(1, 1)
